import numpy as np
import ml_dtypes


def mxq(x, axis, fmt="e4m3"):
    dtype, down = {"e4m3": (ml_dtypes.float8_e4m3fn, 7), "e5m2": (ml_dtypes.float8_e5m2, 14)}[fmt]
    v = np.moveaxis(np.asarray(x, np.float32).astype(ml_dtypes.bfloat16).astype(np.float64), axis, -1)
    blocks = v.reshape(v.shape[:-1] + (-1, 32))
    amax = np.abs(blocks).max(-1, keepdims=True)
    byte = np.maximum(np.where(amax > 0, np.frexp(amax)[1] - 1 + 127, 0) - down, 1)
    scale = np.exp2(byte - 127.0)
    codes = (blocks / scale).astype(np.float32).astype(dtype).astype(np.float64)
    return np.moveaxis((codes * scale).reshape(v.shape), -1, axis)


WIDE = False


def mx_kscale(k):
    if not WIDE:
        return np.ones(k)
    levels = np.array([10, -10, 5, -5, 0])
    if k % 512:
        return np.exp2(np.random.permutation(np.resize(levels, k // 32))).repeat(32)
    a = np.empty((k // 512, 16))
    for p in range(k // 512):
        a[p, :8] = np.random.permutation(np.resize(levels, 8))
        for g in range(8):
            far = levels[np.abs(levels - a[p, g]) >= 10]
            a[p, g + 8] = far[np.random.randint(len(far))]
    return np.exp2(a.ravel()).repeat(32)


def f64(x):
    return np.asarray(x).astype(np.float64)


def striped(idx):
    return np.tile(np.asarray(idx).reshape(-1, 16).T, (8, 1)).astype(np.uint16)


def unstriped(offs):
    return offs[:16].T.reshape(-1).astype(np.int64)


E2M1 = np.array([0.0, 0.5, 1.0, 1.5, 2.0, 3.0, 4.0, 6.0, -0.0, -0.5, -1.0, -1.5, -2.0, -3.0, -4.0, -6.0])


def pack_weight(w, fmt):
    k, n = w.shape
    w = f64(np.asarray(w, np.float32).astype(ml_dtypes.bfloat16)).reshape(k // 32, 32, n)
    amax = np.abs(w).max(1)
    if fmt == "e4m3":
        byte = np.frexp(amax)[1] - 1 + 127 - 7
    else:
        mant, ex = np.frexp(amax / 6.0)
        byte = np.where(mant > 0.5, ex, ex - 1) + 127
    byte = np.clip(np.where(amax > 0, byte, 1), 1, 254)
    scaled = (w * np.exp2(127.0 - byte)[:, None, :]).reshape(k, n).astype(np.float32)
    by_word = np.ascontiguousarray(scaled.reshape(k // 512, 128, 4, n).transpose(0, 1, 3, 2))
    if fmt == "e4m3":
        words = by_word.astype(ml_dtypes.float8_e4m3fn).view(np.uint8)
    else:
        c = by_word.astype(ml_dtypes.float4_e2m1fn).view(np.uint8) & 0xF
        words = (c[..., 0::2] | (c[..., 1::2] << 4)).reshape(k // 512, 128, 2 * n)
    return np.ascontiguousarray(words), np.ascontiguousarray(byte.astype(np.uint8).reshape(k // 512, 16, n))


def unpack_weight(words, scales, fmt):
    g, _, n = scales.shape
    words = np.ascontiguousarray(words).reshape(g, 128, n, -1)
    if fmt == "e4m3":
        vals = words.view(ml_dtypes.float8_e4m3fn).astype(np.float64)
    else:
        nib = np.empty((g, 128, n, 4), np.uint8)
        nib[..., 0::2] = words & 0xF
        nib[..., 1::2] = words >> 4
        vals = E2M1[nib]
    vals = vals * np.repeat(np.exp2(scales.astype(np.float64) - 127.0), 8, axis=1)[..., None]
    return vals.transpose(0, 1, 3, 2).reshape(g * 512, n)


C, I, J, T, R, N = 2048, 512, 512, 512, 512, 512


def setup_inputs():
    n = np.random.standard_normal
    idx = np.random.permutation(C)[:I]
    idx2 = np.random.permutation(C)[:J]
    fi = mx_kscale(I)
    fj = mx_kscale(J)
    fr = mx_kscale(R)
    wap = pack_weight(n((I, R)) * 1 / np.sqrt(I) * fi[:, None] * fr, "e4m3")
    vap = pack_weight(n((R, N)) * 1 / np.sqrt(R) / fr[:, None], "e2m1")
    wbp = pack_weight(n((J, N)) * 1 / np.sqrt(J) * fj[:, None], "e4m3")
    return {
        "xt": (n((T, C))).astype(np.float32),
        "fi": (np.random.uniform(0.5, 2.0, (I, 1)) / fi[:, None]).astype(np.float32),
        "fj": (np.random.uniform(0.5, 2.0, (J, 1)) / fj[:, None]).astype(np.float32),
        "wa_words": wap[0],
        "wa_scales": wap[1],
        "va_words": vap[0],
        "va_scales": vap[1],
        "wb_words": wbp[0],
        "wb_scales": wbp[1],
        "offs": striped(idx),
        "offs2": striped(idx2),
    }


def reference(xt, fi, fj, wa_words, wa_scales, va_words, va_scales, wb_words, wb_scales, offs, offs2):
    idx = unstriped(offs)
    idx2 = unstriped(offs2)
    wau = unpack_weight(wa_words, wa_scales, "e4m3")
    vau = unpack_weight(va_words, va_scales, "e2m1")
    wbu = unpack_weight(wb_words, wb_scales, "e4m3")
    xi = f64(xt)[:, idx].T
    xa = xi * f64(fi)
    xj = f64(xt)[:, idx2].T
    xb = xj * f64(fj)
    xaq = mxq(xa, 0, "e4m3")
    a = wau.T @ xaq
    hid = np.maximum(a, 0.0)
    hidq = mxq(hid, 0, "e4m3")
    xbq = mxq(xb, 0, "e4m3")
    y = vau.T @ hidq + wbu.T @ xbq
    return y

@@ -1,0 +1,190 @@
+from contextlib import ExitStack
+
+import concourse.mybir as mybir
+from concourse.masks import make_identity
+
+C, I, J, T, R, N = 2048, 512, 512, 512, 512, 512
+FLOPS = 2 * T * (I * R + R * N + J * N)
+
+F32 = mybir.dt.float32
+BF16 = mybir.dt.bfloat16
+I32 = mybir.dt.int32
+U32 = mybir.dt.uint32
+U16 = mybir.dt.uint16
+U8 = mybir.dt.uint8
+FP8X4 = mybir.dt.float8_e4m3fn_x4
+FP4X4 = mybir.dt.float4_e2m1fn_x4
+MULT = mybir.AluOpType.mult
+RELU = mybir.ActivationFunctionType.Relu
+
+P = 128
+PACK = 4
+TILES = T // P
+
+
+def tile_list_feature_experts_kernel(tc, xt, fi, fj, wa_words, wa_scales, va_words, va_scales, wb_words, wb_scales, offs, offs2, out):
+    nc = tc.nc
+    with ExitStack() as ctx:
+        keep = ctx.enter_context(tc.tile_pool(name="keep", bufs=1))
+        work = ctx.enter_context(tc.tile_pool(name="work", bufs=3))
+        psum = ctx.enter_context(tc.psum_pool(name="psum", bufs=1))
+
+        def load_scales(queue, plane, scales):
+            for q in range(4):
+                queue.dma_start(plane[32 * q : 32 * q + 4, :].bitcast(I32), scales[0, 4 * q : 4 * q + 4, :].bitcast(I32))
+
+        def load_factor(name, factor):
+            col = keep.tile([P, PACK], F32, name=name)
+            nc.scalar.dma_start(col[:], factor.rearrange("(p j) o -> p (j o)", j=PACK))
+            return col
+
+        planes = keep.tile([P, 3 * N], U8, align_bytes=64)
+        nc.gpsimd.memset(planes[:].bitcast(U32), 0)
+        wa_s_raw, va_s, wb_s = planes[:, 0:R], planes[:, R : R + N], planes[:, R + N :]
+        ident = keep.tile([P, P], F32)
+        make_identity(nc, ident[:])
+
+        fi_col = load_factor("fi_col", fi)
+        fj_col = load_factor("fj_col", fj)
+        load_scales(nc.scalar, wa_s_raw, wa_scales)
+
+        x = [keep.tile([P, C], F32, name="x%d" % k) for k in range(TILES)]
+
+        def load_x(k):
+            nc.sync.dma_start(x[k][:], xt[k * P : (k + 1) * P, :])
+
+        list_a = keep.tile([P, I // 16], U16)
+        nc.sync.dma_start(list_a[:], offs)
+        load_x(0)
+        list_b = keep.tile([P, J // 16], U16)
+        nc.sync.dma_start(list_b[:], offs2)
+        wa_raw = keep.tile([P, R], U32, align_bytes=64)
+        nc.sync.dma_start(wa_raw[:].bitcast(I32), wa_words[0].rearrange("p n t -> p (n t)").bitcast(I32))
+        load_x(1)
+        load_x(2)
+        load_scales(nc.sync, va_s, va_scales)
+        load_x(3)
+        va = keep.tile([P, 2 * N], U8, align_bytes=64)
+        nc.sync.dma_start(va[:].bitcast(I32), va_words[0].bitcast(I32))
+        wb = keep.tile([P, N], U32, align_bytes=64)
+        nc.sync.dma_start(wb[:].bitcast(I32), wb_words[0].rearrange("p n t -> p (n t)").bitcast(I32))
+        load_scales(nc.sync, wb_s, wb_scales)
+
+        def psum_bank(role):
+            return psum.tile([P, PACK, P], F32, name=role, bufs={"turned": 3, "hidden": 2, "result": 3}[role])
+
+        def spread_factor(name, col, copy):
+            bank = psum_bank("turned")
+            for j in range(PACK):
+                nc.tensor.transpose(bank[:, j, :], col[:, j : j + 1].to_broadcast([P, P]), ident[:])
+            row = keep.tile([P, P * PACK], F32, name=name, align_bytes=64)
+            copy(row[:].rearrange("q (p j) -> q p j", j=PACK), bank[:].rearrange("q j p -> q p j"))
+            return row
+
+        fi_row = spread_factor("fi_row", fi_col, nc.vector.tensor_copy)
+        fj_row = spread_factor("fj_row", fj_col, nc.scalar.copy)
+
+        wa = keep.tile([P, R], U32, align_bytes=64)
+        nc.vector.tensor_copy(wa[:].rearrange("p (j m) -> p j m", j=PACK), wa_raw[:].rearrange("p (m j) -> p j m", j=PACK))
+        wa_s = keep.tile([P, R], U8, align_bytes=64)
+        nc.vector.tensor_copy(wa_s[:].rearrange("p (j m) -> p j m", j=PACK), wa_s_raw.rearrange("p (m j) -> p j m", j=PACK))
+
+        def gather(k, offsets, row, name, parts):
+            picked = work.tile([P, P * PACK], F32, name="picked", bufs=2)
+            rounded = work.tile([P, 2, P, 2], BF16, name="rounded", align_bytes=64, bufs=2)
+            for h in range(parts):
+                width = P * PACK // parts
+                cols = slice(h * width, (h + 1) * width)
+                nc.vector.tensor_tensor(picked[:, cols], x[k][:].indirect(offsets[:, h * width // 16 : (h + 1) * width // 16]), row[:, cols], MULT)
+                nc.scalar.copy(rounded[:, :, h * width // PACK : (h + 1) * width // PACK, :], picked[:, cols].rearrange("t (p u e) -> t u p e", u=2, e=2))
+            words = rounded[:].rearrange("t u p e -> t (u p e)").bitcast(F32)
+            bank = psum_bank("turned")
+            for u in range(2):
+                nc.tensor.transpose(bank[:, u, :], words[:, u * P : (u + 1) * P], ident[:])
+            grouped = keep.tile([P, P * PACK], BF16, name="grouped_" + name, align_bytes=64)
+            nc.scalar.copy(grouped[:].bitcast(F32).rearrange("p (t u) -> p t u", u=2), bank[:, 0:2, :].rearrange("p u t -> p t u"))
+            return grouped
+
+        def quantize(name, grouped):
+            codes = keep.tile([P, P], U32, name=name + "_codes", align_bytes=64)
+            scales = keep.tile([P, P], U8, name=name + "_scales", align_bytes=64)
+            nc.vector.quantize_mx(codes[:].bitcast(FP8X4), scales[:], grouped[:])
+            return codes, scales
+
+        def first_layer(xa, on_vector):
+            codes, scales = xa
+            bank = psum_bank("hidden")
+            for j in range(PACK):
+                cols = slice(j * P, (j + 1) * P)
+                nc.tensor.matmul_mx(bank[:, j, :], lhsT=wa[:, cols].bitcast(FP8X4), lhsT_scale=wa_s[:, cols], rhs=codes[:].bitcast(FP8X4), rhs_scale=scales[:], start=True, stop=True)
+            hid = work.tile([P, P * PACK], BF16, name="hid", align_bytes=64, bufs=4)
+            hid_view, bank_view = hid[:].rearrange("p (t j) -> p t j", j=PACK), bank[:].rearrange("p j t -> p t j")
+            if on_vector:
+                nc.vector.tensor_scalar_max(hid_view, bank_view, 0.0)
+            else:
+                nc.scalar.activation(hid_view, bank_view, RELU)
+            return hid
+
+        def open_result(hq, blocks):
+            bank = psum_bank("result")
+            for place, b in enumerate(blocks):
+                nc.tensor.matmul_mx(bank[:, place, :], lhsT=va[:, 2 * b * P : 2 * (b + 1) * P].bitcast(FP4X4), lhsT_scale=va_s[:, b * P : (b + 1) * P], rhs=hq[0][:].bitcast(FP8X4), rhs_scale=hq[1][:], start=(place == 0), stop=False)
+            return bank
+
+        def close_result(k, bank, xb, blocks, copy, queue):
+            for place, b in enumerate(blocks):
+                cols = slice(b * P, (b + 1) * P)
+                nc.tensor.matmul_mx(bank[:, place, :], lhsT=wb[:, cols].bitcast(FP8X4), lhsT_scale=wb_s[:, cols], rhs=xb[0][:].bitcast(FP8X4), rhs_scale=xb[1][:], start=False, stop=(place == len(blocks) - 1))
+            y = work.tile([P, len(blocks), P], F32, name="y", bufs=5)
+            copy(y[:], bank[:, 0 : len(blocks), :])
+            queue.dma_start(out[blocks[0] * P : (blocks[-1] + 1) * P, k * P : (k + 1) * P].rearrange("(b p) t -> p b t", p=P), y[:])
+
+        ga, gb, qa, qb, hid, qh = {}, {}, {}, {}, {}, {}
+
+        def pick_a(k):
+            ga[k] = gather(k, list_a, fi_row, "a%d" % k, 1)
+
+        def pick_b(k, parts=1):
+            gb[k] = gather(k, list_b, fj_row, "b%d" % k, parts)
+
+        def layer_a(k):
+            qa[k] = quantize("xa%d" % k, ga[k])
+            hid[k] = first_layer(qa[k], k == TILES - 1)
+
+        def quant_b(k):
+            qb[k] = quantize("xb%d" % k, gb[k])
+
+        def quant_h(k):
+            qh[k] = quantize("hq%d" % k, hid[k])
+
+        def finish(k):
+            blocks = [0, 1, 2, 3]
+            close_result(k, open_result(qh[k], blocks), qb[k], blocks, nc.scalar.copy, nc.sync)
+
+        pick_a(0)
+        pick_b(0)
+        pick_a(1)
+        layer_a(0)
+        pick_b(1)
+        quant_b(0)
+        pick_a(2)
+        layer_a(1)
+        quant_h(0)
+        pick_a(3)
+        layer_a(2)
+        quant_b(1)
+        finish(0)
+        pick_b(2)
+        layer_a(3)
+        quant_h(1)
+        finish(1)
+        pick_b(3, 2)
+        quant_h(2)
+        quant_b(2)
+        finish(2)
+        quant_h(3)
+        low = open_result(qh[3], [0, 1])
+        high = open_result(qh[3], [2, 3])
+        quant_b(3)
+        close_result(3, low, qb[3], [0, 1], nc.scalar.copy, nc.scalar)
+        close_result(3, high, qb[3], [2, 3], nc.vector.tensor_copy, nc.sync)

@@ -18,6 +18,7 @@ MULT = mybir.AluOpType.mult
 RELU = mybir.ActivationFunctionType.Relu
 
 P = 128
+OPT = {"tag":{"turned":"turned","hidden":"hidden","result":"result"},"bufs":{"turned":3,"hidden":2,"result":3},"pb":2,"rn":"rounded","rb":3,"reluV":[],"yV":[],"dma":["a01","x1","wa","a23","x2","v0123","x3","va","wb","b0123"],"order":["P0","A1","L0","B1","q0","A2","L1","h0","B2","q1","Y0","A3","L2","h1","B3","q2","L3","Y1","h2","Y2"],"parts":2,"hold":{},"pw":"first","ps":"first_r"}
 PACK = 4
 TILES = T // P
 
@@ -29,12 +30,12 @@ def tile_list_feature_experts_kernel(tc, xt, fi, fj, wa_words, wa_scales, va_wor
         work = ctx.enter_context(tc.tile_pool(name="work", bufs=3))
         psum = ctx.enter_context(tc.psum_pool(name="psum", bufs=1))
 
-        def load_scales(queue, plane, scales):
-            for q in range(4):
-                queue.dma_start(plane[32 * q : 32 * q + 4, :].bitcast(I32), scales[0, 4 * q : 4 * q + 4, :].bitcast(I32))
+        def load_scales(plane, scales, quadrants):
+            for q in quadrants:
+                nc.sync.dma_start(plane[32 * q : 32 * q + 4, :].bitcast(I32), scales[0, 4 * q : 4 * q + 4, :].bitcast(I32))
 
         def load_factor(name, factor):
-            col = keep.tile([P, PACK], F32, name=name)
+            col = keep.tile([P, PACK], F32, name=name, align_bytes=64)
             nc.scalar.dma_start(col[:], factor.rearrange("(p j) o -> p (j o)", j=PACK))
             return col
 
@@ -46,7 +47,6 @@ def tile_list_feature_experts_kernel(tc, xt, fi, fj, wa_words, wa_scales, va_wor
 
         fi_col = load_factor("fi_col", fi)
         fj_col = load_factor("fj_col", fj)
-        load_scales(nc.scalar, wa_s_raw, wa_scales)
 
         x = [keep.tile([P, C], F32, name="x%d" % k) for k in range(TILES)]
 
@@ -59,44 +59,49 @@ def tile_list_feature_experts_kernel(tc, xt, fi, fj, wa_words, wa_scales, va_wor
         list_b = keep.tile([P, J // 16], U16)
         nc.sync.dma_start(list_b[:], offs2)
         wa_raw = keep.tile([P, R], U32, align_bytes=64)
-        nc.sync.dma_start(wa_raw[:].bitcast(I32), wa_words[0].rearrange("p n t -> p (n t)").bitcast(I32))
-        load_x(1)
-        load_x(2)
-        load_scales(nc.sync, va_s, va_scales)
-        load_x(3)
         va = keep.tile([P, 2 * N], U8, align_bytes=64)
-        nc.sync.dma_start(va[:].bitcast(I32), va_words[0].bitcast(I32))
         wb = keep.tile([P, N], U32, align_bytes=64)
-        nc.sync.dma_start(wb[:].bitcast(I32), wb_words[0].rearrange("p n t -> p (n t)").bitcast(I32))
-        load_scales(nc.sync, wb_s, wb_scales)
+        for d in OPT["dma"]:
+            if d[0] == "x":
+                load_x(int(d[1]))
+            elif d == "wa":
+                nc.sync.dma_start(wa_raw[:].bitcast(I32), wa_words[0].rearrange("p n t -> p (n t)").bitcast(I32))
+            elif d == "va":
+                nc.sync.dma_start(va[:].bitcast(I32), va_words[0].bitcast(I32))
+            elif d == "wb":
+                nc.sync.dma_start(wb[:].bitcast(I32), wb_words[0].rearrange("p n t -> p (n t)").bitcast(I32))
+            else:
+                load_scales({"a": wa_s_raw, "v": va_s, "b": wb_s}[d[0]], {"a": wa_scales, "v": va_scales, "b": wb_scales}[d[0]], [int(c) for c in d[1:]])
 
         def psum_bank(role):
-            return psum.tile([P, PACK, P], F32, name=role, bufs={"turned": 3, "hidden": 2, "result": 3}[role])
+            return psum.tile([P, PACK, P], F32, name=OPT["tag"][role], bufs=OPT["bufs"][OPT["tag"][role]])
 
         def spread_factor(name, col, copy):
             bank = psum_bank("turned")
             for j in range(PACK):
                 nc.tensor.transpose(bank[:, j, :], col[:, j : j + 1].to_broadcast([P, P]), ident[:])
             row = keep.tile([P, P * PACK], F32, name=name, align_bytes=64)
-            copy(row[:].rearrange("q (p j) -> q p j", j=PACK), bank[:].rearrange("q j p -> q p j"))
+            copy(row[:].rearrange("q (u p e) -> q u p e", u=2, e=2), bank[:].rearrange("q (u e) p -> q u p e", u=2))
             return row
 
-        fi_row = spread_factor("fi_row", fi_col, nc.vector.tensor_copy)
+        fi_row = spread_factor("fi_row", fi_col, nc.scalar.copy)
         fj_row = spread_factor("fj_row", fj_col, nc.scalar.copy)
 
-        wa = keep.tile([P, R], U32, align_bytes=64)
-        nc.vector.tensor_copy(wa[:].rearrange("p (j m) -> p j m", j=PACK), wa_raw[:].rearrange("p (m j) -> p j m", j=PACK))
-        wa_s = keep.tile([P, R], U8, align_bytes=64)
-        nc.vector.tensor_copy(wa_s[:].rearrange("p (j m) -> p j m", j=PACK), wa_s_raw.rearrange("p (m j) -> p j m", j=PACK))
-
         def gather(k, offsets, row, name, parts):
-            picked = work.tile([P, P * PACK], F32, name="picked", bufs=2)
-            rounded = work.tile([P, 2, P, 2], BF16, name="rounded", align_bytes=64, bufs=2)
+            if name == "a0":
+                picked = keep.tile([P, P * PACK], F32, name="first", align_bytes=64)
+            else:
+                picked = work.tile([P, P * PACK], F32, name="staged", align_bytes=64, bufs=OPT["pb"])
+            if name == "a0":
+                rounded = keep.tile([P, 2, P, 2], BF16, name="first_r", align_bytes=64)
+            else:
+                rounded = work.tile([P, 2, P, 2], BF16, name=OPT["rn"], align_bytes=64, bufs=OPT["rb"])
             for h in range(parts):
                 width = P * PACK // parts
                 cols = slice(h * width, (h + 1) * width)
-                nc.vector.tensor_tensor(picked[:, cols], x[k][:].indirect(offsets[:, h * width // 16 : (h + 1) * width // 16]), row[:, cols], MULT)
-                nc.scalar.copy(rounded[:, :, h * width // PACK : (h + 1) * width // PACK, :], picked[:, cols].rearrange("t (p u e) -> t u p e", u=2, e=2))
+                words_h = slice(h * width // PACK, (h + 1) * width // PACK)
+                nc.vector.tensor_copy(picked[:, cols], x[k][:].indirect(offsets[:, h * width // 16 : (h + 1) * width // 16]))
+                nc.gpsimd.tensor_tensor(rounded[:, :, words_h, :], picked[:, cols].rearrange("t (p u e) -> t u p e", u=2, e=2), row[:].rearrange("q (u p e) -> q u p e", u=2, e=2)[:, :, words_h, :], MULT)
             words = rounded[:].rearrange("t u p e -> t (u p e)").bitcast(F32)
             bank = psum_bank("turned")
             for u in range(2):
@@ -105,8 +110,17 @@ def tile_list_feature_experts_kernel(tc, xt, fi, fj, wa_words, wa_scales, va_wor
             nc.scalar.copy(grouped[:].bitcast(F32).rearrange("p (t u) -> p t u", u=2), bank[:, 0:2, :].rearrange("p u t -> p t u"))
             return grouped
 
+        held = {}
+
         def quantize(name, grouped):
-            codes = keep.tile([P, P], U32, name=name + "_codes", align_bytes=64)
+            if name in OPT["hold"]:
+                slot = OPT["hold"][name]
+                if slot not in held:
+                    held[slot] = [keep.tile([P, 4 * P], U32, name=slot, align_bytes=64), 0]
+                codes = held[slot][0][:, held[slot][1] * P : (held[slot][1] + 1) * P]
+                held[slot][1] += 1
+            else:
+                codes = keep.tile([P, P], U32, name=name + "_codes", align_bytes=64)
             scales = keep.tile([P, P], U8, name=name + "_scales", align_bytes=64)
             nc.vector.quantize_mx(codes[:].bitcast(FP8X4), scales[:], grouped[:])
             return codes, scales
@@ -149,7 +163,7 @@ def tile_list_feature_experts_kernel(tc, xt, fi, fj, wa_words, wa_scales, va_wor
 
         def layer_a(k):
             qa[k] = quantize("xa%d" % k, ga[k])
-            hid[k] = first_layer(qa[k], k == TILES - 1)
+            hid[k] = first_layer(qa[k], k in OPT["reluV"])
 
         def quant_b(k):
             qb[k] = quantize("xb%d" % k, gb[k])
@@ -159,29 +173,21 @@ def tile_list_feature_experts_kernel(tc, xt, fi, fj, wa_words, wa_scales, va_wor
 
         def finish(k):
             blocks = [0, 1, 2, 3]
-            close_result(k, open_result(qh[k], blocks), qb[k], blocks, nc.scalar.copy, nc.sync)
+            close_result(k, open_result(qh[k], blocks), qb[k], blocks, nc.vector.tensor_copy if k in OPT["yV"] else nc.scalar.copy, nc.sync)
 
         pick_a(0)
         pick_b(0)
-        pick_a(1)
-        layer_a(0)
-        pick_b(1)
-        quant_b(0)
-        pick_a(2)
-        layer_a(1)
-        quant_h(0)
-        pick_a(3)
-        layer_a(2)
-        quant_b(1)
-        finish(0)
-        pick_b(2)
-        layer_a(3)
-        quant_h(1)
-        finish(1)
-        pick_b(3, 2)
-        quant_h(2)
-        quant_b(2)
-        finish(2)
+        for st in OPT["order"]:
+            k = int(st[1])
+            if st[0] == "P":
+                wa = keep.tile([P, R], U32, name=OPT["pw"], align_bytes=64)
+                nc.vector.tensor_copy(wa[:].rearrange("p (j m) -> p j m", j=PACK), wa_raw[:].rearrange("p (m j) -> p j m", j=PACK))
+                wa_s = keep.tile([P, R], U8, name=OPT["ps"], align_bytes=64)
+                nc.vector.tensor_copy(wa_s[:].rearrange("p (j m) -> p j m", j=PACK), wa_s_raw.rearrange("p (m j) -> p j m", j=PACK))
+            elif st[0] == "B" and k == 3:
+                pick_b(3, OPT["parts"])
+            else:
+                {"A": pick_a, "B": pick_b, "L": layer_a, "q": quant_b, "h": quant_h, "Y": finish}[st[0]](k)
         quant_h(3)
         low = open_result(qh[3], [0, 1])
         high = open_result(qh[3], [2, 3])

@@ -18,179 +18,193 @@ MULT = mybir.AluOpType.mult
 RELU = mybir.ActivationFunctionType.Relu
 
 P = 128
-OPT = {"tag":{"turned":"turned","hidden":"hidden","result":"result"},"bufs":{"turned":3,"hidden":2,"result":3},"pb":2,"rn":"rounded","rb":3,"reluV":[],"yV":[],"dma":["a01","x1","wa","a23","x2","v0123","x3","va","wb","b0123"],"order":["P0","A1","L0","B1","q0","A2","L1","h0","B2","q1","Y0","A3","L2","h1","B3","q2","L3","Y1","h2","Y2"],"parts":2,"hold":{},"pw":"first","ps":"first_r"}
 PACK = 4
+K = P * PACK
 TILES = T // P
+BLOCKS = N // P
+ALIGN = 64
+BANKS = {"turned": 3, "hidden": 2, "result": 3}
 
 
-def tile_list_feature_experts_kernel(tc, xt, fi, fj, wa_words, wa_scales, va_words, va_scales, wb_words, wb_scales, offs, offs2, out):
+def tile_list_feature_experts_kernel(
+    tc, xt, fi, fj, wa_words, wa_scales, va_words, va_scales, wb_words, wb_scales, offs, offs2, out
+):
     nc = tc.nc
     with ExitStack() as ctx:
         keep = ctx.enter_context(tc.tile_pool(name="keep", bufs=1))
-        work = ctx.enter_context(tc.tile_pool(name="work", bufs=3))
+        ring = ctx.enter_context(tc.tile_pool(name="ring", bufs=2))
         psum = ctx.enter_context(tc.psum_pool(name="psum", bufs=1))
 
-        def load_scales(plane, scales, quadrants):
-            for q in quadrants:
-                nc.sync.dma_start(plane[32 * q : 32 * q + 4, :].bitcast(I32), scales[0, 4 * q : 4 * q + 4, :].bitcast(I32))
+        def buffer(name, shape, dtype):
+            return keep.tile(shape, dtype, name=name, align_bytes=ALIGN)
 
-        def load_factor(name, factor):
-            col = keep.tile([P, PACK], F32, name=name, align_bytes=64)
-            nc.scalar.dma_start(col[:], factor.rearrange("(p j) o -> p (j o)", j=PACK))
-            return col
+        def psum_bank(role):
+            return psum.tile([P, PACK, P], F32, name=role, bufs=BANKS[role])
 
-        planes = keep.tile([P, 3 * N], U8, align_bytes=64)
+        planes = buffer("planes", [P, R + 2 * N], U8)
         nc.gpsimd.memset(planes[:].bitcast(U32), 0)
-        wa_s_raw, va_s, wb_s = planes[:, 0:R], planes[:, R : R + N], planes[:, R + N :]
+        wa_scale_raw, va_scale, wb_scale = planes[:, 0:R], planes[:, R : R + N], planes[:, R + N :]
         ident = keep.tile([P, P], F32)
         make_identity(nc, ident[:])
 
-        fi_col = load_factor("fi_col", fi)
-        fj_col = load_factor("fj_col", fj)
+        def load_factor(name, factor):
+            col = buffer(name, [P, PACK], F32)
+            nc.scalar.dma_start(col[:], factor.rearrange("(p c) o -> p (c o)", c=PACK))
+            return col
 
-        x = [keep.tile([P, C], F32, name="x%d" % k) for k in range(TILES)]
+        def load_scales(plane, scales, quadrants):
+            for q in quadrants:
+                nc.sync.dma_start(
+                    plane[32 * q : 32 * q + 4, :].bitcast(I32), scales[0, 4 * q : 4 * q + 4, :].bitcast(I32)
+                )
 
-        def load_x(k):
+        def load_tokens(k):
             nc.sync.dma_start(x[k][:], xt[k * P : (k + 1) * P, :])
 
-        list_a = keep.tile([P, I // 16], U16)
-        nc.sync.dma_start(list_a[:], offs)
-        load_x(0)
-        list_b = keep.tile([P, J // 16], U16)
-        nc.sync.dma_start(list_b[:], offs2)
-        wa_raw = keep.tile([P, R], U32, align_bytes=64)
-        va = keep.tile([P, 2 * N], U8, align_bytes=64)
-        wb = keep.tile([P, N], U32, align_bytes=64)
-        for d in OPT["dma"]:
-            if d[0] == "x":
-                load_x(int(d[1]))
-            elif d == "wa":
-                nc.sync.dma_start(wa_raw[:].bitcast(I32), wa_words[0].rearrange("p n t -> p (n t)").bitcast(I32))
-            elif d == "va":
-                nc.sync.dma_start(va[:].bitcast(I32), va_words[0].bitcast(I32))
-            elif d == "wb":
-                nc.sync.dma_start(wb[:].bitcast(I32), wb_words[0].rearrange("p n t -> p (n t)").bitcast(I32))
-            else:
-                load_scales({"a": wa_s_raw, "v": va_s, "b": wb_s}[d[0]], {"a": wa_scales, "v": va_scales, "b": wb_scales}[d[0]], [int(c) for c in d[1:]])
+        def load_words(tile, words):
+            nc.sync.dma_start(tile[:].bitcast(I32), words.bitcast(I32))
 
-        def psum_bank(role):
-            return psum.tile([P, PACK, P], F32, name=OPT["tag"][role], bufs=OPT["bufs"][OPT["tag"][role]])
+        fi_col = load_factor("fi_col", fi)
+        fj_col = load_factor("fj_col", fj)
+        x = [buffer("x%d" % k, [P, C], F32) for k in range(TILES)]
+        list_a = keep.tile([P, I // 16], U16)
+        list_b = keep.tile([P, J // 16], U16)
+        wa_raw = buffer("wa_raw", [P, R], U32)
+        va = buffer("va", [P, 2 * N], U8)
+        wb = buffer("wb", [P, N], U32)
+
+        nc.sync.dma_start(list_a[:], offs)
+        load_tokens(0)
+        nc.sync.dma_start(list_b[:], offs2)
+        load_words(wa_raw, wa_words[0].rearrange("p n c -> p (n c)"))
+        load_scales(wa_scale_raw, wa_scales, (0, 1))
+        load_tokens(1)
+        load_scales(wa_scale_raw, wa_scales, (2, 3))
+        load_tokens(2)
+        load_scales(va_scale, va_scales, range(4))
+        load_tokens(3)
+        load_words(va, va_words[0])
+        load_words(wb, wb_words[0].rearrange("p n c -> p (n c)"))
+        load_scales(wb_scale, wb_scales, range(4))
 
         def spread_factor(name, col, copy):
             bank = psum_bank("turned")
-            for j in range(PACK):
-                nc.tensor.transpose(bank[:, j, :], col[:, j : j + 1].to_broadcast([P, P]), ident[:])
-            row = keep.tile([P, P * PACK], F32, name=name, align_bytes=64)
-            copy(row[:].rearrange("q (u p e) -> q u p e", u=2, e=2), bank[:].rearrange("q (u e) p -> q u p e", u=2))
+            for c in range(PACK):
+                nc.tensor.transpose(bank[:, c, :], col[:, c : c + 1].to_broadcast([P, P]), ident[:])
+            row = buffer(name, [P, K], F32)
+            copy(row[:].rearrange("t (p c) -> t p c", c=PACK), bank[:].rearrange("t c p -> t p c"))
             return row
 
-        fi_row = spread_factor("fi_row", fi_col, nc.scalar.copy)
+        fi_row = spread_factor("fi_row", fi_col, nc.vector.tensor_copy)
         fj_row = spread_factor("fj_row", fj_col, nc.scalar.copy)
 
-        def gather(k, offsets, row, name, parts):
-            if name == "a0":
-                picked = keep.tile([P, P * PACK], F32, name="first", align_bytes=64)
-            else:
-                picked = work.tile([P, P * PACK], F32, name="staged", align_bytes=64, bufs=OPT["pb"])
-            if name == "a0":
-                rounded = keep.tile([P, 2, P, 2], BF16, name="first_r", align_bytes=64)
-            else:
-                rounded = work.tile([P, 2, P, 2], BF16, name=OPT["rn"], align_bytes=64, bufs=OPT["rb"])
-            for h in range(parts):
-                width = P * PACK // parts
-                cols = slice(h * width, (h + 1) * width)
-                words_h = slice(h * width // PACK, (h + 1) * width // PACK)
-                nc.vector.tensor_copy(picked[:, cols], x[k][:].indirect(offsets[:, h * width // 16 : (h + 1) * width // 16]))
-                nc.gpsimd.tensor_tensor(rounded[:, :, words_h, :], picked[:, cols].rearrange("t (p u e) -> t u p e", u=2, e=2), row[:].rearrange("q (u p e) -> q u p e", u=2, e=2)[:, :, words_h, :], MULT)
+        def pick(k, offsets, row, name, picked_in, rounded, copy):
+            picked = buffer(picked_in, [P, K], F32)
+            nc.vector.tensor_tensor(picked[:], x[k][:].indirect(offsets[:]), row[:], MULT)
+            copy(rounded[:], picked[:].rearrange("t (p u e) -> t u p e", u=2, e=2))
             words = rounded[:].rearrange("t u p e -> t (u p e)").bitcast(F32)
             bank = psum_bank("turned")
             for u in range(2):
                 nc.tensor.transpose(bank[:, u, :], words[:, u * P : (u + 1) * P], ident[:])
-            grouped = keep.tile([P, P * PACK], BF16, name="grouped_" + name, align_bytes=64)
-            nc.scalar.copy(grouped[:].bitcast(F32).rearrange("p (t u) -> p t u", u=2), bank[:, 0:2, :].rearrange("p u t -> p t u"))
+            grouped = buffer("grouped_" + name, [P, K], BF16)
+            copy(grouped[:].bitcast(F32).rearrange("p (t u) -> p t u", u=2), bank[:, 0:2, :].rearrange("p u t -> p t u"))
             return grouped
 
-        held = {}
+        def rounded_ring():
+            return ring.tile([P, 2, P, 2], BF16, name="rounded", align_bytes=ALIGN)
 
-        def quantize(name, grouped):
-            if name in OPT["hold"]:
-                slot = OPT["hold"][name]
-                if slot not in held:
-                    held[slot] = [keep.tile([P, 4 * P], U32, name=slot, align_bytes=64), 0]
-                codes = held[slot][0][:, held[slot][1] * P : (held[slot][1] + 1) * P]
-                held[slot][1] += 1
-            else:
-                codes = keep.tile([P, P], U32, name=name + "_codes", align_bytes=64)
-            scales = keep.tile([P, P], U8, name=name + "_scales", align_bytes=64)
-            nc.vector.quantize_mx(codes[:].bitcast(FP8X4), scales[:], grouped[:])
-            return codes, scales
+        def rounded_in(name):
+            return buffer(name, [P, 2, P, 2], BF16)
 
-        def first_layer(xa, on_vector):
-            codes, scales = xa
+        def codes_in(name, count):
+            tile = buffer(name, [P, count * P], U32)
+            return [tile[:, n * P : (n + 1) * P] for n in range(count)]
+
+        def quantize(name, grouped, codes):
+            scales = buffer(name + "_scales", [P, P], U8)
+            nc.vector.quantize_mx(codes.bitcast(FP8X4), scales[:], grouped[:])
+            return codes.bitcast(FP8X4), scales[:]
+
+        def first_layer(k, xa):
             bank = psum_bank("hidden")
-            for j in range(PACK):
-                cols = slice(j * P, (j + 1) * P)
-                nc.tensor.matmul_mx(bank[:, j, :], lhsT=wa[:, cols].bitcast(FP8X4), lhsT_scale=wa_s[:, cols], rhs=codes[:].bitcast(FP8X4), rhs_scale=scales[:], start=True, stop=True)
-            hid = work.tile([P, P * PACK], BF16, name="hid", align_bytes=64, bufs=4)
-            hid_view, bank_view = hid[:].rearrange("p (t j) -> p t j", j=PACK), bank[:].rearrange("p j t -> p t j")
-            if on_vector:
-                nc.vector.tensor_scalar_max(hid_view, bank_view, 0.0)
-            else:
-                nc.scalar.activation(hid_view, bank_view, RELU)
+            for c in range(PACK):
+                cols = slice(c * P, (c + 1) * P)
+                nc.tensor.matmul_mx(
+                    bank[:, c, :], lhsT=wa[:, cols].bitcast(FP8X4), lhsT_scale=wa_scale[:, cols],
+                    rhs=xa[0], rhs_scale=xa[1], start=True, stop=True,
+                )
+            hid = buffer("hid%d" % k, [P, K], BF16)
+            nc.scalar.activation(hid[:].rearrange("p (t c) -> p t c", c=PACK), bank[:].rearrange("p c t -> p t c"), RELU)
             return hid
 
         def open_result(hq, blocks):
             bank = psum_bank("result")
             for place, b in enumerate(blocks):
-                nc.tensor.matmul_mx(bank[:, place, :], lhsT=va[:, 2 * b * P : 2 * (b + 1) * P].bitcast(FP4X4), lhsT_scale=va_s[:, b * P : (b + 1) * P], rhs=hq[0][:].bitcast(FP8X4), rhs_scale=hq[1][:], start=(place == 0), stop=False)
+                nc.tensor.matmul_mx(
+                    bank[:, place, :], lhsT=va[:, 2 * b * P : 2 * (b + 1) * P].bitcast(FP4X4),
+                    lhsT_scale=va_scale[:, b * P : (b + 1) * P],
+                    rhs=hq[0], rhs_scale=hq[1], start=(place == 0), stop=False,
+                )
             return bank
 
         def close_result(k, bank, xb, blocks, copy, queue):
             for place, b in enumerate(blocks):
                 cols = slice(b * P, (b + 1) * P)
-                nc.tensor.matmul_mx(bank[:, place, :], lhsT=wb[:, cols].bitcast(FP8X4), lhsT_scale=wb_s[:, cols], rhs=xb[0][:].bitcast(FP8X4), rhs_scale=xb[1][:], start=False, stop=(place == len(blocks) - 1))
-            y = work.tile([P, len(blocks), P], F32, name="y", bufs=5)
+                nc.tensor.matmul_mx(
+                    bank[:, place, :], lhsT=wb[:, cols].bitcast(FP8X4), lhsT_scale=wb_scale[:, cols],
+                    rhs=xb[0], rhs_scale=xb[1], start=False, stop=(place == len(blocks) - 1),
+                )
+            y = buffer("y%d_%d" % (k, blocks[0]), [P, len(blocks), P], F32)
             copy(y[:], bank[:, 0 : len(blocks), :])
-            queue.dma_start(out[blocks[0] * P : (blocks[-1] + 1) * P, k * P : (k + 1) * P].rearrange("(b p) t -> p b t", p=P), y[:])
+            rows = slice(blocks[0] * P, (blocks[-1] + 1) * P)
+            queue.dma_start(out[rows, k * P : (k + 1) * P].rearrange("(b p) t -> p b t", p=P), y[:])
 
-        ga, gb, qa, qb, hid, qh = {}, {}, {}, {}, {}, {}
+        def second_layer(k, hq, xb):
+            blocks = range(BLOCKS)
+            close_result(k, open_result(hq, blocks), xb, blocks, nc.scalar.copy, nc.sync)
 
-        def pick_a(k):
-            ga[k] = gather(k, list_a, fi_row, "a%d" % k, 1)
+        scalar_copy, vector_copy = nc.scalar.copy, nc.vector.tensor_copy
+        a0 = pick(0, list_a, fi_row, "a0", "picked_a0", rounded_in("rounded_a0"), scalar_copy)
+        b0 = pick(0, list_b, fj_row, "b0", "picked_b0", rounded_ring(), scalar_copy)
 
-        def pick_b(k, parts=1):
-            gb[k] = gather(k, list_b, fj_row, "b%d" % k, parts)
+        wa = buffer("picked_a0", [P, R], U32)
+        nc.vector.tensor_copy(wa[:].rearrange("p (c m) -> p c m", c=PACK), wa_raw[:].rearrange("p (m c) -> p c m", c=PACK))
+        wa_scale = buffer("rounded_a0", [P, R], U8)
+        nc.vector.tensor_copy(
+            wa_scale[:].rearrange("p (c m) -> p c m", c=PACK), wa_scale_raw.rearrange("p (m c) -> p c m", c=PACK)
+        )
 
-        def layer_a(k):
-            qa[k] = quantize("xa%d" % k, ga[k])
-            hid[k] = first_layer(qa[k], k in OPT["reluV"])
+        a1 = pick(1, list_a, fi_row, "a1", "picked_a1", rounded_ring(), scalar_copy)
+        b1 = pick(1, list_b, fj_row, "b1", "picked_b1", rounded_ring(), scalar_copy)
+        behind_b1 = codes_in("x1", 2)
+        hid0 = first_layer(0, quantize("xa0", a0, behind_b1[0]))
+        xb0 = quantize("xb0", b0, behind_b1[1])
 
-        def quant_b(k):
-            qb[k] = quantize("xb%d" % k, gb[k])
+        a2 = pick(2, list_a, fi_row, "a2", "picked_a2", rounded_ring(), scalar_copy)
+        a3 = pick(3, list_a, fi_row, "a3", "picked_a3", rounded_in("rounded_a3"), scalar_copy)
+        behind_a3 = codes_in("fi_row", 4)
+        hid1 = first_layer(1, quantize("xa1", a1, behind_a3[0]))
+        hq0 = quantize("hq0", hid0, behind_a3[1])
+        xb1 = quantize("xb1", b1, behind_a3[2])
+        hid2 = first_layer(2, quantize("xa2", a2, behind_a3[3]))
+        second_layer(0, hq0, xb0)
 
-        def quant_h(k):
-            qh[k] = quantize("hq%d" % k, hid[k])
+        b2 = pick(2, list_b, fj_row, "b2", "grouped_a1", rounded_in("rounded_a3"), scalar_copy)
+        behind_b2 = codes_in("x2", 2)
+        hid3 = first_layer(3, quantize("xa3", a3, behind_b2[0]))
+        hq1 = quantize("hq1", hid1, behind_b2[1])
+        second_layer(1, hq1, xb1)
 
-        def finish(k):
-            blocks = [0, 1, 2, 3]
-            close_result(k, open_result(qh[k], blocks), qb[k], blocks, nc.vector.tensor_copy if k in OPT["yV"] else nc.scalar.copy, nc.sync)
+        b3 = pick(3, list_b, fj_row, "b3", "grouped_a3", rounded_ring(), vector_copy)
+        behind_b3 = codes_in("x3", 2)
+        hq2 = quantize("hq2", hid2, behind_b3[0])
+        xb2 = quantize("xb2", b2, behind_b3[1])
+        second_layer(2, hq2, xb2)
 
-        pick_a(0)
-        pick_b(0)
-        for st in OPT["order"]:
-            k = int(st[1])
-            if st[0] == "P":
-                wa = keep.tile([P, R], U32, name=OPT["pw"], align_bytes=64)
-                nc.vector.tensor_copy(wa[:].rearrange("p (j m) -> p j m", j=PACK), wa_raw[:].rearrange("p (m j) -> p j m", j=PACK))
-                wa_s = keep.tile([P, R], U8, name=OPT["ps"], align_bytes=64)
-                nc.vector.tensor_copy(wa_s[:].rearrange("p (j m) -> p j m", j=PACK), wa_s_raw.rearrange("p (m j) -> p j m", j=PACK))
-            elif st[0] == "B" and k == 3:
-                pick_b(3, OPT["parts"])
-            else:
-                {"A": pick_a, "B": pick_b, "L": layer_a, "q": quant_b, "h": quant_h, "Y": finish}[st[0]](k)
-        quant_h(3)
-        low = open_result(qh[3], [0, 1])
-        high = open_result(qh[3], [2, 3])
-        quant_b(3)
-        close_result(3, low, qb[3], [0, 1], nc.scalar.copy, nc.scalar)
-        close_result(3, high, qb[3], [2, 3], nc.vector.tensor_copy, nc.sync)
+        hq3 = quantize("hq3", hid3, codes_in("hq3_codes", 1)[0])
+        low, high = range(0, BLOCKS // 2), range(BLOCKS // 2, BLOCKS)
+        low_bank = open_result(hq3, low)
+        high_bank = open_result(hq3, high)
+        xb3 = quantize("xb3", b3, codes_in("xb3_codes", 1)[0])
+        close_result(3, low_bank, xb3, low, scalar_copy, nc.scalar)
+        close_result(3, high_bank, xb3, high, vector_copy, nc.sync)

@@ -52,9 +52,9 @@ def tile_list_feature_experts_kernel(
             nc.scalar.dma_start(col[:], factor.rearrange("(p c) o -> p (c o)", c=PACK))
             return col
 
-        def load_scales(plane, scales, quadrants):
-            for q in quadrants:
-                nc.sync.dma_start(
+        def load_scales(queue, plane, scales):
+            for q in range(4):
+                queue.dma_start(
                     plane[32 * q : 32 * q + 4, :].bitcast(I32), scales[0, 4 * q : 4 * q + 4, :].bitcast(I32)
                 )
 
@@ -66,6 +66,7 @@ def tile_list_feature_experts_kernel(
 
         fi_col = load_factor("fi_col", fi)
         fj_col = load_factor("fj_col", fj)
+        load_scales(nc.scalar, wa_scale_raw, wa_scales)
         x = [buffer("x%d" % k, [P, C], F32) for k in range(TILES)]
         list_a = keep.tile([P, I // 16], U16)
         list_b = keep.tile([P, J // 16], U16)
@@ -77,15 +78,13 @@ def tile_list_feature_experts_kernel(
         load_tokens(0)
         nc.sync.dma_start(list_b[:], offs2)
         load_words(wa_raw, wa_words[0].rearrange("p n c -> p (n c)"))
-        load_scales(wa_scale_raw, wa_scales, (0, 1))
         load_tokens(1)
-        load_scales(wa_scale_raw, wa_scales, (2, 3))
         load_tokens(2)
-        load_scales(va_scale, va_scales, range(4))
+        load_scales(nc.sync, va_scale, va_scales)
         load_tokens(3)
         load_words(va, va_words[0])
         load_words(wb, wb_words[0].rearrange("p n c -> p (n c)"))
-        load_scales(wb_scale, wb_scales, range(4))
+        load_scales(nc.sync, wb_scale, wb_scales)
 
         def spread_factor(name, col, copy):
             bank = psum_bank("turned")
@@ -98,8 +97,8 @@ def tile_list_feature_experts_kernel(
         fi_row = spread_factor("fi_row", fi_col, nc.vector.tensor_copy)
         fj_row = spread_factor("fj_row", fj_col, nc.scalar.copy)
 
-        def pick(k, offsets, row, name, picked_in, rounded, copy):
-            picked = buffer(picked_in, [P, K], F32)
+        def pick(k, offsets, row, name, staging, copy):
+            picked, rounded = staging
             nc.vector.tensor_tensor(picked[:], x[k][:].indirect(offsets[:]), row[:], MULT)
             copy(rounded[:], picked[:].rearrange("t (p u e) -> t u p e", u=2, e=2))
             words = rounded[:].rearrange("t u p e -> t (u p e)").bitcast(F32)
@@ -110,20 +109,16 @@ def tile_list_feature_experts_kernel(
             copy(grouped[:].bitcast(F32).rearrange("p (t u) -> p t u", u=2), bank[:, 0:2, :].rearrange("p u t -> p t u"))
             return grouped
 
-        def rounded_ring():
-            return ring.tile([P, 2, P, 2], BF16, name="rounded", align_bytes=ALIGN)
+        def staging_ring():
+            picked = ring.tile([P, K], F32, name="picked", align_bytes=ALIGN)
+            rounded = ring.tile([P, 2, P, 2], BF16, name="rounded", align_bytes=ALIGN)
+            return picked, rounded
 
-        def rounded_in(name):
-            return buffer(name, [P, 2, P, 2], BF16)
-
-        def codes_in(name, count):
-            tile = buffer(name, [P, count * P], U32)
-            return [tile[:, n * P : (n + 1) * P] for n in range(count)]
-
-        def quantize(name, grouped, codes):
+        def quantize(name, grouped):
+            codes = buffer(name + "_codes", [P, P], U32)
             scales = buffer(name + "_scales", [P, P], U8)
-            nc.vector.quantize_mx(codes.bitcast(FP8X4), scales[:], grouped[:])
-            return codes.bitcast(FP8X4), scales[:]
+            nc.vector.quantize_mx(codes[:].bitcast(FP8X4), scales[:], grouped[:])
+            return codes[:].bitcast(FP8X4), scales[:]
 
         def first_layer(k, xa):
             bank = psum_bank("hidden")
@@ -164,8 +159,9 @@ def tile_list_feature_experts_kernel(
             close_result(k, open_result(hq, blocks), xb, blocks, nc.scalar.copy, nc.sync)
 
         scalar_copy, vector_copy = nc.scalar.copy, nc.vector.tensor_copy
-        a0 = pick(0, list_a, fi_row, "a0", "picked_a0", rounded_in("rounded_a0"), scalar_copy)
-        b0 = pick(0, list_b, fj_row, "b0", "picked_b0", rounded_ring(), scalar_copy)
+        first_staging = buffer("picked_a0", [P, K], F32), buffer("rounded_a0", [P, 2, P, 2], BF16)
+        a0 = pick(0, list_a, fi_row, "a0", first_staging, scalar_copy)
+        b0 = pick(0, list_b, fj_row, "b0", staging_ring(), scalar_copy)
 
         wa = buffer("picked_a0", [P, R], U32)
         nc.vector.tensor_copy(wa[:].rearrange("p (c m) -> p c m", c=PACK), wa_raw[:].rearrange("p (m c) -> p c m", c=PACK))
@@ -174,37 +170,30 @@ def tile_list_feature_experts_kernel(
             wa_scale[:].rearrange("p (c m) -> p c m", c=PACK), wa_scale_raw.rearrange("p (m c) -> p c m", c=PACK)
         )
 
-        a1 = pick(1, list_a, fi_row, "a1", "picked_a1", rounded_ring(), scalar_copy)
-        b1 = pick(1, list_b, fj_row, "b1", "picked_b1", rounded_ring(), scalar_copy)
-        behind_b1 = codes_in("x1", 2)
-        hid0 = first_layer(0, quantize("xa0", a0, behind_b1[0]))
-        xb0 = quantize("xb0", b0, behind_b1[1])
-
-        a2 = pick(2, list_a, fi_row, "a2", "picked_a2", rounded_ring(), scalar_copy)
-        a3 = pick(3, list_a, fi_row, "a3", "picked_a3", rounded_in("rounded_a3"), scalar_copy)
-        behind_a3 = codes_in("fi_row", 4)
-        hid1 = first_layer(1, quantize("xa1", a1, behind_a3[0]))
-        hq0 = quantize("hq0", hid0, behind_a3[1])
-        xb1 = quantize("xb1", b1, behind_a3[2])
-        hid2 = first_layer(2, quantize("xa2", a2, behind_a3[3]))
+        a1 = pick(1, list_a, fi_row, "a1", staging_ring(), scalar_copy)
+        hid0 = first_layer(0, quantize("xa0", a0))
+        b1 = pick(1, list_b, fj_row, "b1", staging_ring(), scalar_copy)
+        xb0 = quantize("xb0", b0)
+        a2 = pick(2, list_a, fi_row, "a2", staging_ring(), scalar_copy)
+        hid1 = first_layer(1, quantize("xa1", a1))
+        hq0 = quantize("hq0", hid0)
+        a3 = pick(3, list_a, fi_row, "a3", staging_ring(), scalar_copy)
+        hid2 = first_layer(2, quantize("xa2", a2))
+        xb1 = quantize("xb1", b1)
         second_layer(0, hq0, xb0)
-
-        b2 = pick(2, list_b, fj_row, "b2", "grouped_a1", rounded_in("rounded_a3"), scalar_copy)
-        behind_b2 = codes_in("x2", 2)
-        hid3 = first_layer(3, quantize("xa3", a3, behind_b2[0]))
-        hq1 = quantize("hq1", hid1, behind_b2[1])
+        b2 = pick(2, list_b, fj_row, "b2", staging_ring(), scalar_copy)
+        hid3 = first_layer(3, quantize("xa3", a3))
+        hq1 = quantize("hq1", hid1)
         second_layer(1, hq1, xb1)
-
-        b3 = pick(3, list_b, fj_row, "b3", "grouped_a3", rounded_ring(), vector_copy)
-        behind_b3 = codes_in("x3", 2)
-        hq2 = quantize("hq2", hid2, behind_b3[0])
-        xb2 = quantize("xb2", b2, behind_b3[1])
+        b3 = pick(3, list_b, fj_row, "b3", staging_ring(), vector_copy)
+        hq2 = quantize("hq2", hid2)
+        xb2 = quantize("xb2", b2)
         second_layer(2, hq2, xb2)
 
-        hq3 = quantize("hq3", hid3, codes_in("hq3_codes", 1)[0])
+        hq3 = quantize("hq3", hid3)
         low, high = range(0, BLOCKS // 2), range(BLOCKS // 2, BLOCKS)
         low_bank = open_result(hq3, low)
         high_bank = open_result(hq3, high)
-        xb3 = quantize("xb3", b3, codes_in("xb3_codes", 1)[0])
+        xb3 = quantize("xb3", b3)
         close_result(3, low_bank, xb3, low, scalar_copy, nc.scalar)
         close_result(3, high_bank, xb3, high, vector_copy, nc.sync)

@@ -165,7 +165,7 @@ def tile_list_feature_experts_kernel(
 
         wa = buffer("picked_a0", [P, R], U32)
         nc.vector.tensor_copy(wa[:].rearrange("p (c m) -> p c m", c=PACK), wa_raw[:].rearrange("p (m c) -> p c m", c=PACK))
-        wa_scale = buffer("rounded_a0", [P, R], U8)
+        wa_scale = buffer("fi_col", [P, R], U8)
         nc.vector.tensor_copy(
             wa_scale[:].rearrange("p (c m) -> p c m", c=PACK), wa_scale_raw.rearrange("p (m c) -> p c m", c=PACK)
         )

from contextlib import ExitStack

import concourse.mybir as mybir
from concourse.masks import make_identity

C, I, J, T, R, N = 2048, 512, 512, 512, 512, 512
FLOPS = 2 * T * (I * R + R * N + J * N)

F32 = mybir.dt.float32
BF16 = mybir.dt.bfloat16
I32 = mybir.dt.int32
U32 = mybir.dt.uint32
U16 = mybir.dt.uint16
U8 = mybir.dt.uint8
FP8X4 = mybir.dt.float8_e4m3fn_x4
FP4X4 = mybir.dt.float4_e2m1fn_x4
MULT = mybir.AluOpType.mult
RELU = mybir.ActivationFunctionType.Relu

P = 128
PACK = 4
K = P * PACK
TILES = T // P
BLOCKS = N // P
ALIGN = 64
BANKS = {"turned": 3, "hidden": 2, "result": 3}


def tile_list_feature_experts_kernel(
    tc, xt, fi, fj, wa_words, wa_scales, va_words, va_scales, wb_words, wb_scales, offs, offs2, out
):
    nc = tc.nc
    with ExitStack() as ctx:
        keep = ctx.enter_context(tc.tile_pool(name="keep", bufs=1))
        ring = ctx.enter_context(tc.tile_pool(name="ring", bufs=2))
        psum = ctx.enter_context(tc.psum_pool(name="psum", bufs=1))

        def buffer(name, shape, dtype):
            return keep.tile(shape, dtype, name=name, align_bytes=ALIGN)

        def psum_bank(role):
            return psum.tile([P, PACK, P], F32, name=role, bufs=BANKS[role])

        planes = buffer("planes", [P, R + 2 * N], U8)
        nc.gpsimd.memset(planes[:].bitcast(U32), 0)
        wa_scale_raw, va_scale, wb_scale = planes[:, 0:R], planes[:, R : R + N], planes[:, R + N :]
        ident = keep.tile([P, P], F32)
        make_identity(nc, ident[:])

        def load_factor(name, factor):
            col = buffer(name, [P, PACK], F32)
            nc.scalar.dma_start(col[:], factor.rearrange("(p c) o -> p (c o)", c=PACK))
            return col

        def load_scales(queue, plane, scales):
            for q in range(4):
                queue.dma_start(
                    plane[32 * q : 32 * q + 4, :].bitcast(I32), scales[0, 4 * q : 4 * q + 4, :].bitcast(I32)
                )

        def load_tokens(k):
            nc.sync.dma_start(x[k][:], xt[k * P : (k + 1) * P, :])

        def load_words(tile, words):
            nc.sync.dma_start(tile[:].bitcast(I32), words.bitcast(I32))

        fi_col = load_factor("fi_col", fi)
        fj_col = load_factor("fj_col", fj)
        load_scales(nc.scalar, wa_scale_raw, wa_scales)
        x = [buffer("x%d" % k, [P, C], F32) for k in range(TILES)]
        list_a = keep.tile([P, I // 16], U16)
        list_b = keep.tile([P, J // 16], U16)
        wa_raw = buffer("wa_raw", [P, R], U32)
        va = buffer("va", [P, 2 * N], U8)
        wb = buffer("wb", [P, N], U32)

        nc.sync.dma_start(list_a[:], offs)
        load_tokens(0)
        nc.sync.dma_start(list_b[:], offs2)
        load_words(wa_raw, wa_words[0].rearrange("p n c -> p (n c)"))
        load_tokens(1)
        load_tokens(2)
        load_scales(nc.sync, va_scale, va_scales)
        load_tokens(3)
        load_words(va, va_words[0])
        load_words(wb, wb_words[0].rearrange("p n c -> p (n c)"))
        load_scales(nc.sync, wb_scale, wb_scales)

        def spread_factor(name, col, copy):
            bank = psum_bank("turned")
            for c in range(PACK):
                nc.tensor.transpose(bank[:, c, :], col[:, c : c + 1].to_broadcast([P, P]), ident[:])
            row = buffer(name, [P, K], F32)
            copy(row[:].rearrange("t (p c) -> t p c", c=PACK), bank[:].rearrange("t c p -> t p c"))
            return row

        fi_row = spread_factor("fi_row", fi_col, nc.vector.tensor_copy)
        fj_row = spread_factor("fj_row", fj_col, nc.scalar.copy)

        def pick(k, offsets, row, name, staging, copy):
            picked, rounded = staging
            nc.vector.tensor_tensor(picked[:], x[k][:].indirect(offsets[:]), row[:], MULT)
            copy(rounded[:], picked[:].rearrange("t (p u e) -> t u p e", u=2, e=2))
            words = rounded[:].rearrange("t u p e -> t (u p e)").bitcast(F32)
            bank = psum_bank("turned")
            for u in range(2):
                nc.tensor.transpose(bank[:, u, :], words[:, u * P : (u + 1) * P], ident[:])
            grouped = buffer("grouped_" + name, [P, K], BF16)
            copy(grouped[:].bitcast(F32).rearrange("p (t u) -> p t u", u=2), bank[:, 0:2, :].rearrange("p u t -> p t u"))
            return grouped

        def staging_ring():
            picked = ring.tile([P, K], F32, name="picked", align_bytes=ALIGN)
            rounded = ring.tile([P, 2, P, 2], BF16, name="rounded", align_bytes=ALIGN)
            return picked, rounded

        def quantize(name, grouped):
            codes = buffer(name + "_codes", [P, P], U32)
            scales = buffer(name + "_scales", [P, P], U8)
            nc.vector.quantize_mx(codes[:].bitcast(FP8X4), scales[:], grouped[:])
            return codes[:].bitcast(FP8X4), scales[:]

        def first_layer(k, xa):
            bank = psum_bank("hidden")
            for c in range(PACK):
                cols = slice(c * P, (c + 1) * P)
                nc.tensor.matmul_mx(
                    bank[:, c, :], lhsT=wa[:, cols].bitcast(FP8X4), lhsT_scale=wa_scale[:, cols],
                    rhs=xa[0], rhs_scale=xa[1], start=True, stop=True,
                )
            hid = buffer("hid%d" % k, [P, K], BF16)
            nc.scalar.activation(hid[:].rearrange("p (t c) -> p t c", c=PACK), bank[:].rearrange("p c t -> p t c"), RELU)
            return hid

        def open_result(hq, blocks):
            bank = psum_bank("result")
            for place, b in enumerate(blocks):
                nc.tensor.matmul_mx(
                    bank[:, place, :], lhsT=va[:, 2 * b * P : 2 * (b + 1) * P].bitcast(FP4X4),
                    lhsT_scale=va_scale[:, b * P : (b + 1) * P],
                    rhs=hq[0], rhs_scale=hq[1], start=(place == 0), stop=False,
                )
            return bank

        def close_result(k, bank, xb, blocks, copy, queue):
            for place, b in enumerate(blocks):
                cols = slice(b * P, (b + 1) * P)
                nc.tensor.matmul_mx(
                    bank[:, place, :], lhsT=wb[:, cols].bitcast(FP8X4), lhsT_scale=wb_scale[:, cols],
                    rhs=xb[0], rhs_scale=xb[1], start=False, stop=(place == len(blocks) - 1),
                )
            y = buffer("y%d_%d" % (k, blocks[0]), [P, len(blocks), P], F32)
            copy(y[:], bank[:, 0 : len(blocks), :])
            rows = slice(blocks[0] * P, (blocks[-1] + 1) * P)
            queue.dma_start(out[rows, k * P : (k + 1) * P].rearrange("(b p) t -> p b t", p=P), y[:])

        def second_layer(k, hq, xb):
            blocks = range(BLOCKS)
            close_result(k, open_result(hq, blocks), xb, blocks, nc.scalar.copy, nc.sync)

        scalar_copy, vector_copy = nc.scalar.copy, nc.vector.tensor_copy
        first_staging = buffer("picked_a0", [P, K], F32), buffer("rounded_a0", [P, 2, P, 2], BF16)
        a0 = pick(0, list_a, fi_row, "a0", first_staging, scalar_copy)
        b0 = pick(0, list_b, fj_row, "b0", staging_ring(), scalar_copy)

        wa = buffer("picked_a0", [P, R], U32)
        nc.vector.tensor_copy(wa[:].rearrange("p (c m) -> p c m", c=PACK), wa_raw[:].rearrange("p (m c) -> p c m", c=PACK))
        wa_scale = buffer("fi_col", [P, R], U8)
        nc.vector.tensor_copy(
            wa_scale[:].rearrange("p (c m) -> p c m", c=PACK), wa_scale_raw.rearrange("p (m c) -> p c m", c=PACK)
        )

        a1 = pick(1, list_a, fi_row, "a1", staging_ring(), scalar_copy)
        hid0 = first_layer(0, quantize("xa0", a0))
        b1 = pick(1, list_b, fj_row, "b1", staging_ring(), scalar_copy)
        xb0 = quantize("xb0", b0)
        a2 = pick(2, list_a, fi_row, "a2", staging_ring(), scalar_copy)
        hid1 = first_layer(1, quantize("xa1", a1))
        hq0 = quantize("hq0", hid0)
        a3 = pick(3, list_a, fi_row, "a3", staging_ring(), scalar_copy)
        hid2 = first_layer(2, quantize("xa2", a2))
        xb1 = quantize("xb1", b1)
        second_layer(0, hq0, xb0)
        b2 = pick(2, list_b, fj_row, "b2", staging_ring(), scalar_copy)
        hid3 = first_layer(3, quantize("xa3", a3))
        hq1 = quantize("hq1", hid1)
        second_layer(1, hq1, xb1)
        b3 = pick(3, list_b, fj_row, "b3", staging_ring(), vector_copy)
        hq2 = quantize("hq2", hid2)
        xb2 = quantize("xb2", b2)
        second_layer(2, hq2, xb2)

        hq3 = quantize("hq3", hid3)
        low, high = range(0, BLOCKS // 2), range(BLOCKS // 2, BLOCKS)
        low_bank = open_result(hq3, low)
        high_bank = open_result(hq3, high)
        xb3 = quantize("xb3", b3)
        close_result(3, low_bank, xb3, low, scalar_copy, nc.scalar)
        close_result(3, high_bank, xb3, high, vector_copy, nc.sync)
